import numpy as np, ml_dtypes
CORES = [2,3,42,43,82,83,122,123]
N = 8
TK = 64
def setup_inputs(rng):
    return {"b": rng.standard_normal((N, 128, TK), dtype=np.float32).astype(ml_dtypes.bfloat16), "l": (rng.standard_normal((N, 128, N * 128), dtype=np.float32) / 16).astype(ml_dtypes.bfloat16)}
def setup_inputs_big(rng):
    d = setup_inputs(rng)
    for k in ("b",): d[k] = (d[k].astype(np.float32) * 1048576.0).astype(d[k].dtype)
    return d
def setup_inputs_small(rng):
    d = setup_inputs(rng)
    for k in ("b",): d[k] = (d[k].astype(np.float32) * (1 / 1048576.0)).astype(d[k].dtype)
    return d
def setup_inputs_apart(rng):
    d = setup_inputs(rng)
    f = (10.0 ** rng.permutation(np.linspace(-1.5, 1.5, N))).astype(np.float32).reshape(N, 1, 1)
    for k in ("b",): d[k] = (d[k].astype(np.float32) * f).astype(d[k].dtype)
    return d
def reference(b, l):
    B, L = b.astype(np.float64), l.astype(np.float64)
    y = np.zeros((N, 128, TK))
    for r in range(N):
        acc = B[r].copy()
        for s in range(r):
            acc -= L[s][:, 128 * r:128 * r + 128].T @ y[s]
        y[r] = acc
    return {"y": y.astype(ml_dtypes.bfloat16)}

@@ -1,0 +1,229 @@
+from concourse.mybir import AluOpType
+
+N = 8
+TK = 64
+TS = 128
+W = TK + (N - 1) * TS
+L1 = 4
+SOLVERS = {4: 4, 5: 5, 6: 6, 7: 7}
+
+SCRATCH = {
+    "own": ("sbuf", [128, W], "bfloat16"),
+    "ybuf": ("sbuf", [128, N * TK], "bfloat16"),
+    "qsrc": ("sbuf", [128, (N - L1) * TK], "bfloat16"),
+    "qin": ("sbuf", [128, (N - L1) * TK], "bfloat16"),
+    "p0": ("sbuf", [128, (N - L1) * TK], "float32"),
+    "ebuf": ("sbuf", [128, (N - L1) * TK], "float32"),
+    "ps0": ("psum", [128, 512], "float32"),
+    "ps1": ("psum", [128, 512], "float32"),
+    "ps2": ("psum", [128, 512], "float32"),
+    "ps3": ("psum", [128, 512], "float32"),
+}
+for _s in range(N - 1):
+    SCRATCH["in%d" % _s] = ("sbuf", [128, W], "bfloat16")
+
+SEMAPHORES = (["ld0", "ld1", "ld2", "st", "snt", "a0b", "aq", "ay", "mq0", "mq1", "pc", "qs"]
+              + ["a%d" % s for s in range(N - 1)]
+              + ["mm%d" % r for r in range(1, N)]
+              + ["yr%d" % r for r in range(1, N)]
+              + ["er%d" % r for r in range(L1, N)])
+
+
+def _col(r, s):
+    return TK + TS * (r - s - 1)
+
+
+def rank_program(g, core, T, topo):
+    me = T.rank_of(core)
+    if me is None:
+        return
+    cores = T.cores
+    sem = T.sem
+    sent = [0]
+    seen = {}
+    queues = {"g": g, "t": g.tensor, "v": g.vector, "sy": g.sync, "sc": g.scalar}
+
+    def width(src, dst):
+        return bin(topo.mask(cores[src], cores[dst])).count("1")
+
+    def wait(q, name, val):
+        if seen.get((q, name), 0) >= val:
+            return
+        seen[(q, name)] = val
+        queues[q].wait_ge(sem[name], val)
+
+    def send(dst, out_ap, in_ap, name):
+        rid, pid, _ = topo.addr(cores[dst])
+        m = topo.mask(core, cores[dst])
+        g.remote_dma(out_ap, in_ap, remote_sem=sem[name], local_sem=sem.snt, pid=pid, routing_id=rid,
+                     dma_engine_mask=m)
+        sent[0] += bin(m).count("1")
+
+    def blk(s):
+        return T.own if s == me else T["in%d" % s]
+
+    def tile(r, s):
+        return blk(s)[:, _col(r, s):_col(r, s) + TS]
+
+    def bvec(s):
+        return blk(s)[:, 0:TK]
+
+    def yv(s):
+        return T.ybuf[:, TK * s:TK * (s + 1)]
+
+    def bank(r):
+        return T["ps%d" % (r % 4)]
+
+    def ready(q, r, s):
+        if s == me:
+            wait(q, "ld0" if r is None else ("ld1" if r < L1 else "ld2"), 16)
+        elif s == 0 and r is not None and r >= L1:
+            wait(q, "a0b", width(s, me))
+        else:
+            wait(q, "a%d" % s, width(s, me))
+
+    def block_to(dst, c0, c1, name):
+        send(dst, T["in%d" % me][:, c0:c1], T.own[:, c0:c1], name)
+
+    def mm(r, s, rhs, start, stop):
+        g.tensor.matmul(bank(r)[:, 0:TK], tile(r, s), rhs, start=start, stop=stop).then_inc(sem["mm%d" % r], 1)
+
+    def store(q, src):
+        queues[q].dma_start(T.y[:, :], src).then_inc(sem.st, 16)
+        wait(q, "st", 16)
+
+    loaded = ["ld0"]
+    g.sync.dma_start(T.own[:, 0:TK], T.b[:, :]).then_inc(sem.ld0, 16)
+    if me + 1 < L1:
+        g.scalar.dma_start(T.own[:, _col(me + 1, me):_col(L1, me)], T.l[:, TS * (me + 1):TS * L1]).then_inc(sem.ld1, 16)
+        loaded.append("ld1")
+    r0 = max(L1, me + 1)
+    if r0 < N:
+        q2 = g.sync if me + 1 < L1 else g.scalar
+        q2.dma_start(T.own[:, _col(r0, me):_col(N, me)], T.l[:, TS * r0:TS * N]).then_inc(sem.ld2, 16)
+        loaded.append("ld2")
+
+    order = sorted(SOLVERS, key=lambda k: -SOLVERS[k])
+
+    if me == 0:
+        wait("g", "ld0", 16)
+        wait("g", "ld1", 16)
+        block_to(1, 0, _col(2, 0), "a0")
+        wait("g", "ld2", 16)
+        block_to(1, _col(L1, 0), _col(N, 0), "a0b")
+        wait("sc", "ld0", 16)
+        store("sc", T.own[:, 0:TK])
+        for s in range(0, L1 - 1):
+            for r in range(s + 1, L1):
+                ready("t", r, s)
+                if s == 0:
+                    ready("t", None, 0)
+                    rhs = bvec(0)
+                else:
+                    wait("t", "yr%d" % s, 1)
+                    rhs = yv(s)
+                mm(r, s, rhs, s == 0, s == r - 1)
+        for r in range(1, L1):
+            ready("v", None, r)
+            wait("v", "mm%d" % r, r)
+            g.vector.tensor_tensor(yv(r), bvec(r), bank(r)[:, 0:TK], AluOpType.subtract).then_inc(sem["yr%d" % r], 1)
+        wait("g", "yr2", 1)
+        wait("g", "yr3", 1)
+        for d in order:
+            send(d, T.ybuf[:, 2 * TK:4 * TK], T.ybuf[:, 2 * TK:4 * TK], "ay")
+        send(3, yv(3), yv(3), "ay")
+        send(2, yv(2), yv(2), "ay")
+
+    elif me == 1:
+        wait("g", "ld0", 16)
+        wait("g", "ld1", 16)
+        block_to(0, 0, _col(L1, 1), "a1")
+        nq = N - L1
+        ready("t", 1, 0)
+        mm(1, 0, bvec(0), True, True)
+        ready("v", None, 1)
+        wait("v", "mm1", 1)
+        g.vector.tensor_tensor(yv(1), bvec(1), bank(1)[:, 0:TK], AluOpType.subtract).then_inc(sem.yr1, 1)
+        wait("sy", "yr1", 1)
+        store("sy", yv(1))
+        for r in range(L1, N):
+            ready("t", r, 0)
+            k = r - L1
+            g.tensor.matmul(T.ps2[:, TK * k:TK * (k + 1)], tile(r, 0), bvec(0), start=True, stop=True).then_inc(sem.mq0, 1)
+        wait("v", "mq0", nq)
+        g.vector.tensor_copy(T.p0[:, :], T.ps2[:, 0:TK * nq]).then_inc(sem.pc, 1)
+        wait("t", "yr1", 1)
+        for r in range(L1, N):
+            ready("t", r, 1)
+            k = r - L1
+            g.tensor.matmul(T.ps3[:, TK * k:TK * (k + 1)], tile(r, 1), yv(1), start=True, stop=True).then_inc(sem.mq1, 1)
+        wait("v", "mq1", nq)
+        wait("v", "pc", 1)
+        g.vector.tensor_tensor(T.qsrc[:, :], T.p0[:, :], T.ps3[:, 0:TK * nq], AluOpType.add).then_inc(sem.qs, 1)
+        wait("g", "qs", 1)
+        for d in order:
+            c = TK * (SOLVERS[d] - L1 + 1)
+            send(d, T.qin[:, 0:c], T.qsrc[:, 0:c], "aq")
+
+    elif me < L1:
+        wait("g", "ld0", 16)
+        if me + 1 < L1:
+            wait("g", "ld1", 16)
+        block_to(0, 0, _col(L1, me), "a%d" % me)
+        wait("g", "ld2", 16)
+        for d in order:
+            block_to(d, _col(L1, me), _col(SOLVERS[d] + 1, me), "a%d" % me)
+        wait("sy", "ay", width(0, me))
+        store("sy", yv(me))
+
+    else:
+        for d in order:
+            if d != me and SOLVERS[d] >= me:
+                wait("g", "ld0", 16)
+                if SOLVERS[d] > me:
+                    wait("g", "ld2", 16)
+                block_to(d, 0, _col(SOLVERS[d] + 1, me), "a%d" % me)
+        if me in SOLVERS:
+            top = SOLVERS[me]
+            wait("t", "ay", width(0, me))
+            for r in range(L1, top + 1):
+                for s in range(2, r):
+                    ready("t", r, s)
+                    if s >= L1:
+                        wait("t", "yr%d" % s, 1)
+                    mm(r, s, yv(s), s == 2, s == r - 1)
+
+            def e_op(r):
+                k = r - L1
+                ready("v", None, r)
+                wait("v", "aq", width(1, me))
+                g.vector.tensor_tensor(T.ebuf[:, TK * k:TK * (k + 1)], bvec(r), T.qin[:, TK * k:TK * (k + 1)],
+                                       AluOpType.subtract).then_inc(sem["er%d" % r], 1)
+
+            def y_op(r):
+                k = r - L1
+                wait("v", "er%d" % r, 1)
+                wait("v", "mm%d" % r, r - 2)
+                g.vector.tensor_tensor(yv(r), T.ebuf[:, TK * k:TK * (k + 1)], bank(r)[:, 0:TK],
+                                       AluOpType.subtract).then_inc(sem["yr%d" % r], 1)
+
+            e_op(L1)
+            for r in range(L1, top + 1):
+                if r + 1 <= top:
+                    e_op(r + 1)
+                y_op(r)
+            wait("sy", "yr%d" % me, 1)
+            store("sy", yv(me))
+            for r in range(top, L1 - 1, -1):
+                if r != me and r not in SOLVERS:
+                    wait("g", "yr%d" % r, 1)
+                    send(r, yv(r), yv(r), "ay")
+        else:
+            src = [d for d in SOLVERS if SOLVERS[d] >= me][0]
+            wait("sy", "ay", width(src, me))
+            store("sy", yv(me))
+
+    for name in loaded:
+        wait("g", name, 16)
+    if sent[0]:
+        wait("g", "snt", sent[0])

@@ -4,8 +4,8 @@ N = 8
 TK = 64
 TS = 128
 W = TK + (N - 1) * TS
-L1 = 4
-SOLVERS = {4: 4, 5: 5, 6: 6, 7: 7}
+L1 = 5
+SOLVERS = {r: r for r in range(L1, N)}
 
 SCRATCH = {
     "own": ("sbuf", [128, W], "bfloat16"),
@@ -14,11 +14,9 @@ SCRATCH = {
     "qin": ("sbuf", [128, (N - L1) * TK], "bfloat16"),
     "p0": ("sbuf", [128, (N - L1) * TK], "float32"),
     "ebuf": ("sbuf", [128, (N - L1) * TK], "float32"),
-    "ps0": ("psum", [128, 512], "float32"),
-    "ps1": ("psum", [128, 512], "float32"),
-    "ps2": ("psum", [128, 512], "float32"),
-    "ps3": ("psum", [128, 512], "float32"),
 }
+for _s in range(N):
+    SCRATCH["ps%d" % _s] = ("psum", [128, 512], "float32")
 for _s in range(N - 1):
     SCRATCH["in%d" % _s] = ("sbuf", [128, W], "bfloat16")
 
@@ -72,7 +70,7 @@ def rank_program(g, core, T, topo):
         return T.ybuf[:, TK * s:TK * (s + 1)]
 
     def bank(r):
-        return T["ps%d" % (r % 4)]
+        return T["ps%d" % r]
 
     def ready(q, r, s):
         if s == me:
@@ -127,12 +125,12 @@ def rank_program(g, core, T, topo):
             ready("v", None, r)
             wait("v", "mm%d" % r, r)
             g.vector.tensor_tensor(yv(r), bvec(r), bank(r)[:, 0:TK], AluOpType.subtract).then_inc(sem["yr%d" % r], 1)
-        wait("g", "yr2", 1)
-        wait("g", "yr3", 1)
+        for r in range(2, L1):
+            wait("g", "yr%d" % r, 1)
         for d in order:
-            send(d, T.ybuf[:, 2 * TK:4 * TK], T.ybuf[:, 2 * TK:4 * TK], "ay")
-        send(3, yv(3), yv(3), "ay")
-        send(2, yv(2), yv(2), "ay")
+            send(d, T.ybuf[:, 2 * TK:L1 * TK], T.ybuf[:, 2 * TK:L1 * TK], "ay")
+        for r in range(L1 - 1, 1, -1):
+            send(r, yv(r), yv(r), "ay")
 
     elif me == 1:
         wait("g", "ld0", 16)
@@ -183,45 +181,36 @@ def rank_program(g, core, T, topo):
                 if SOLVERS[d] > me:
                     wait("g", "ld2", 16)
                 block_to(d, 0, _col(SOLVERS[d] + 1, me), "a%d" % me)
-        if me in SOLVERS:
-            top = SOLVERS[me]
-            wait("t", "ay", width(0, me))
-            for r in range(L1, top + 1):
-                for s in range(2, r):
-                    ready("t", r, s)
-                    if s >= L1:
-                        wait("t", "yr%d" % s, 1)
-                    mm(r, s, yv(s), s == 2, s == r - 1)
+        top = SOLVERS[me]
+        wait("t", "ay", width(0, me))
+        for r in range(L1, top + 1):
+            for s in range(2, r):
+                ready("t", r, s)
+                if s >= L1:
+                    wait("t", "yr%d" % s, 1)
+                mm(r, s, yv(s), s == 2, s == r - 1)
 
-            def e_op(r):
-                k = r - L1
-                ready("v", None, r)
-                wait("v", "aq", width(1, me))
-                g.vector.tensor_tensor(T.ebuf[:, TK * k:TK * (k + 1)], bvec(r), T.qin[:, TK * k:TK * (k + 1)],
-                                       AluOpType.subtract).then_inc(sem["er%d" % r], 1)
+        def e_op(r):
+            k = r - L1
+            ready("v", None, r)
+            wait("v", "aq", width(1, me))
+            g.vector.tensor_tensor(T.ebuf[:, TK * k:TK * (k + 1)], bvec(r), T.qin[:, TK * k:TK * (k + 1)],
+                                   AluOpType.subtract).then_inc(sem["er%d" % r], 1)
 
-            def y_op(r):
-                k = r - L1
-                wait("v", "er%d" % r, 1)
-                wait("v", "mm%d" % r, r - 2)
-                g.vector.tensor_tensor(yv(r), T.ebuf[:, TK * k:TK * (k + 1)], bank(r)[:, 0:TK],
-                                       AluOpType.subtract).then_inc(sem["yr%d" % r], 1)
+        def y_op(r):
+            k = r - L1
+            wait("v", "er%d" % r, 1)
+            wait("v", "mm%d" % r, r - 2)
+            g.vector.tensor_tensor(yv(r), T.ebuf[:, TK * k:TK * (k + 1)], bank(r)[:, 0:TK],
+                                   AluOpType.subtract).then_inc(sem["yr%d" % r], 1)
 
-            e_op(L1)
-            for r in range(L1, top + 1):
-                if r + 1 <= top:
-                    e_op(r + 1)
-                y_op(r)
-            wait("sy", "yr%d" % me, 1)
-            store("sy", yv(me))
-            for r in range(top, L1 - 1, -1):
-                if r != me and r not in SOLVERS:
-                    wait("g", "yr%d" % r, 1)
-                    send(r, yv(r), yv(r), "ay")
-        else:
-            src = [d for d in SOLVERS if SOLVERS[d] >= me][0]
-            wait("sy", "ay", width(src, me))
-            store("sy", yv(me))
+        e_op(L1)
+        for r in range(L1, top + 1):
+            if r + 1 <= top:
+                e_op(r + 1)
+            y_op(r)
+        wait("sy", "yr%d" % me, 1)
+        store("sy", yv(me))
 
     for name in loaded:
         wait("g", name, 16)

@@ -4,8 +4,9 @@ N = 8
 TK = 64
 TS = 128
 W = TK + (N - 1) * TS
-L1 = 5
-SOLVERS = {r: r for r in range(L1, N)}
+LS = 4
+L1 = 6
+SOLVERS = list(range(N - 1, L1 - 1, -1))
 
 SCRATCH = {
     "own": ("sbuf", [128, W], "bfloat16"),
@@ -20,8 +21,9 @@ for _s in range(N):
 for _s in range(N - 1):
     SCRATCH["in%d" % _s] = ("sbuf", [128, W], "bfloat16")
 
-SEMAPHORES = (["ld0", "ld1", "ld2", "st", "snt", "a0b", "aq", "ay", "mq0", "mq1", "pc", "qs"]
+SEMAPHORES = (["ld0", "ld1", "ld2", "ld3", "st", "snt", "a0b", "aq", "ay", "ay2", "mq0", "mq1", "pc", "qs"]
               + ["a%d" % s for s in range(N - 1)]
+              + ["c%d" % s for s in range(2, LS)]
               + ["mm%d" % r for r in range(1, N)]
               + ["yr%d" % r for r in range(1, N)]
               + ["er%d" % r for r in range(L1, N)])
@@ -69,22 +71,34 @@ def rank_program(g, core, T, topo):
     def yv(s):
         return T.ybuf[:, TK * s:TK * (s + 1)]
 
+    def ys(a, b):
+        return T.ybuf[:, TK * a:TK * b]
+
     def bank(r):
         return T["ps%d" % r]
 
+    def ld_of(r):
+        return "ld1" if r < LS else ("ld3" if r < L1 else "ld2")
+
     def ready(q, r, s):
         if s == me:
-            wait(q, "ld0" if r is None else ("ld1" if r < L1 else "ld2"), 16)
+            wait(q, "ld0" if r is None else ld_of(r), 16)
         elif s == 0 and r is not None and r >= L1:
             wait(q, "a0b", width(s, me))
+        elif me == 0 and 2 <= s < LS and r is not None and r >= LS:
+            wait(q, "c%d" % s, width(s, me))
         else:
             wait(q, "a%d" % s, width(s, me))
 
     def block_to(dst, c0, c1, name):
         send(dst, T["in%d" % me][:, c0:c1], T.own[:, c0:c1], name)
 
-    def mm(r, s, rhs, start, stop):
-        g.tensor.matmul(bank(r)[:, 0:TK], tile(r, s), rhs, start=start, stop=stop).then_inc(sem["mm%d" % r], 1)
+    count = {}
+
+    def mm(r, s, rhs, total):
+        count[r] = count.get(r, 0) + 1
+        g.tensor.matmul(bank(r)[:, 0:TK], tile(r, s), rhs, start=count[r] == 1,
+                        stop=count[r] == total).then_inc(sem["mm%d" % r], 1)
 
     def store(q, src):
         queues[q].dma_start(T.y[:, :], src).then_inc(sem.st, 16)
@@ -92,16 +106,14 @@ def rank_program(g, core, T, topo):
 
     loaded = ["ld0"]
     g.sync.dma_start(T.own[:, 0:TK], T.b[:, :]).then_inc(sem.ld0, 16)
-    if me + 1 < L1:
-        g.scalar.dma_start(T.own[:, _col(me + 1, me):_col(L1, me)], T.l[:, TS * (me + 1):TS * L1]).then_inc(sem.ld1, 16)
-        loaded.append("ld1")
-    r0 = max(L1, me + 1)
-    if r0 < N:
-        q2 = g.sync if me + 1 < L1 else g.scalar
-        q2.dma_start(T.own[:, _col(r0, me):_col(N, me)], T.l[:, TS * r0:TS * N]).then_inc(sem.ld2, 16)
-        loaded.append("ld2")
-
-    order = sorted(SOLVERS, key=lambda k: -SOLVERS[k])
+    nld = 0
+    for lo, hi in ((1, LS), (LS, L1), (L1, N)):
+        r0 = max(lo, me + 1)
+        if r0 < hi:
+            q = g.scalar if nld % 2 == 0 else g.sync
+            nld += 1
+            q.dma_start(T.own[:, _col(r0, me):_col(hi, me)], T.l[:, TS * r0:TS * hi]).then_inc(sem[ld_of(r0)], 16)
+            loaded.append(ld_of(r0))
 
     if me == 0:
         wait("g", "ld0", 16)
@@ -111,34 +123,38 @@ def rank_program(g, core, T, topo):
         block_to(1, _col(L1, 0), _col(N, 0), "a0b")
         wait("sc", "ld0", 16)
         store("sc", T.own[:, 0:TK])
-        for s in range(0, L1 - 1):
-            for r in range(s + 1, L1):
-                ready("t", r, s)
-                if s == 0:
-                    ready("t", None, 0)
-                    rhs = bvec(0)
-                else:
-                    wait("t", "yr%d" % s, 1)
-                    rhs = yv(s)
-                mm(r, s, rhs, s == 0, s == r - 1)
+        for lo, hi in ((1, LS), (LS, L1)):
+            cols = [s for s in (0, 1) if s < lo] + list(range(lo - 1, 1, -1)) + list(range(lo, hi - 1))
+            for s in cols:
+                for r in range(max(lo, s + 1), hi):
+                    ready("t", r, s)
+                    if s == 0:
+                        ready("t", None, 0)
+                        rhs = bvec(0)
+                    else:
+                        wait("t", "yr%d" % s, 1)
+                        rhs = yv(s)
+                    mm(r, s, rhs, r)
         for r in range(1, L1):
             ready("v", None, r)
             wait("v", "mm%d" % r, r)
             g.vector.tensor_tensor(yv(r), bvec(r), bank(r)[:, 0:TK], AluOpType.subtract).then_inc(sem["yr%d" % r], 1)
-        for r in range(2, L1):
-            wait("g", "yr%d" % r, 1)
-        for d in order:
-            send(d, T.ybuf[:, 2 * TK:L1 * TK], T.ybuf[:, 2 * TK:L1 * TK], "ay")
-        for r in range(L1 - 1, 1, -1):
-            send(r, yv(r), yv(r), "ay")
+        for lo, hi, name in ((2, LS, "ay"), (LS, L1, "ay2")):
+            for r in range(lo, hi):
+                wait("g", "yr%d" % r, 1)
+            for d in SOLVERS:
+                send(d, ys(lo, hi), ys(lo, hi), name)
+            for r in range(hi - 1, lo - 1, -1):
+                send(r, yv(r), yv(r), "ay")
 
     elif me == 1:
         wait("g", "ld0", 16)
         wait("g", "ld1", 16)
+        wait("g", "ld3", 16)
         block_to(0, 0, _col(L1, 1), "a1")
         nq = N - L1
         ready("t", 1, 0)
-        mm(1, 0, bvec(0), True, True)
+        mm(1, 0, bvec(0), 1)
         ready("v", None, 1)
         wait("v", "mm1", 1)
         g.vector.tensor_tensor(yv(1), bvec(1), bank(1)[:, 0:TK], AluOpType.subtract).then_inc(sem.yr1, 1)
@@ -159,36 +175,40 @@ def rank_program(g, core, T, topo):
         wait("v", "pc", 1)
         g.vector.tensor_tensor(T.qsrc[:, :], T.p0[:, :], T.ps3[:, 0:TK * nq], AluOpType.add).then_inc(sem.qs, 1)
         wait("g", "qs", 1)
-        for d in order:
-            c = TK * (SOLVERS[d] - L1 + 1)
+        for d in SOLVERS:
+            c = TK * (d - L1 + 1)
             send(d, T.qin[:, 0:c], T.qsrc[:, 0:c], "aq")
 
     elif me < L1:
         wait("g", "ld0", 16)
-        if me + 1 < L1:
-            wait("g", "ld1", 16)
-        block_to(0, 0, _col(L1, me), "a%d" % me)
+        if me < LS:
+            if me + 1 < LS:
+                wait("g", "ld1", 16)
+            block_to(0, 0, _col(LS, me), "a%d" % me)
+            wait("g", "ld3", 16)
+            block_to(0, _col(LS, me), _col(L1, me), "c%d" % me)
+        else:
+            if me + 1 < L1:
+                wait("g", "ld3", 16)
+            block_to(0, 0, _col(L1, me), "a%d" % me)
         wait("g", "ld2", 16)
-        for d in order:
-            block_to(d, _col(L1, me), _col(SOLVERS[d] + 1, me), "a%d" % me)
+        for d in SOLVERS:
+            block_to(d, _col(L1, me), _col(d + 1, me), "a%d" % me)
         wait("sy", "ay", width(0, me))
         store("sy", yv(me))
 
     else:
-        for d in order:
-            if d != me and SOLVERS[d] >= me:
+        for d in SOLVERS:
+            if d > me:
                 wait("g", "ld0", 16)
-                if SOLVERS[d] > me:
-                    wait("g", "ld2", 16)
-                block_to(d, 0, _col(SOLVERS[d] + 1, me), "a%d" % me)
-        top = SOLVERS[me]
-        wait("t", "ay", width(0, me))
-        for r in range(L1, top + 1):
-            for s in range(2, r):
-                ready("t", r, s)
-                if s >= L1:
-                    wait("t", "yr%d" % s, 1)
-                mm(r, s, yv(s), s == 2, s == r - 1)
+                wait("g", "ld2", 16)
+                block_to(d, 0, _col(d + 1, me), "a%d" % me)
+        rows = range(L1, me + 1)
+        todo = [(r, s) for s in range(2, LS) for r in rows] + [(r, s) for r in rows for s in range(LS, r)]
+        for r, s in todo:
+            wait("t", "ay" if s < LS else ("ay2" if s < L1 else "yr%d" % s), width(0, me) if s < L1 else 1)
+            ready("t", r, s)
+            mm(r, s, yv(s), r - 2)
 
         def e_op(r):
             k = r - L1
@@ -205,8 +225,8 @@ def rank_program(g, core, T, topo):
                                    AluOpType.subtract).then_inc(sem["yr%d" % r], 1)
 
         e_op(L1)
-        for r in range(L1, top + 1):
-            if r + 1 <= top:
+        for r in rows:
+            if r + 1 <= me:
                 e_op(r + 1)
             y_op(r)
         wait("sy", "yr%d" % me, 1)

from concourse.mybir import AluOpType

N = 8
TK = 64
TS = 128
W = TK + (N - 1) * TS
LS = 4
L1 = 6
SOLVERS = list(range(N - 1, L1 - 1, -1))

SCRATCH = {
    "own": ("sbuf", [128, W], "bfloat16"),
    "ybuf": ("sbuf", [128, N * TK], "bfloat16"),
    "qsrc": ("sbuf", [128, (N - L1) * TK], "bfloat16"),
    "qin": ("sbuf", [128, (N - L1) * TK], "bfloat16"),
    "p0": ("sbuf", [128, (N - L1) * TK], "float32"),
    "ebuf": ("sbuf", [128, (N - L1) * TK], "float32"),
}
for _s in range(N):
    SCRATCH["ps%d" % _s] = ("psum", [128, 512], "float32")
for _s in range(N - 1):
    SCRATCH["in%d" % _s] = ("sbuf", [128, W], "bfloat16")

SEMAPHORES = (["ld0", "ld1", "ld2", "ld3", "st", "snt", "a0b", "aq", "ay", "ay2", "mq0", "mq1", "pc", "qs"]
              + ["a%d" % s for s in range(N - 1)]
              + ["c%d" % s for s in range(2, LS)]
              + ["mm%d" % r for r in range(1, N)]
              + ["yr%d" % r for r in range(1, N)]
              + ["er%d" % r for r in range(L1, N)])


def _col(r, s):
    return TK + TS * (r - s - 1)


def rank_program(g, core, T, topo):
    me = T.rank_of(core)
    if me is None:
        return
    cores = T.cores
    sem = T.sem
    sent = [0]
    seen = {}
    queues = {"g": g, "t": g.tensor, "v": g.vector, "sy": g.sync, "sc": g.scalar}

    def width(src, dst):
        return bin(topo.mask(cores[src], cores[dst])).count("1")

    def wait(q, name, val):
        if seen.get((q, name), 0) >= val:
            return
        seen[(q, name)] = val
        queues[q].wait_ge(sem[name], val)

    def send(dst, out_ap, in_ap, name):
        rid, pid, _ = topo.addr(cores[dst])
        m = topo.mask(core, cores[dst])
        g.remote_dma(out_ap, in_ap, remote_sem=sem[name], local_sem=sem.snt, pid=pid, routing_id=rid,
                     dma_engine_mask=m)
        sent[0] += bin(m).count("1")

    def blk(s):
        return T.own if s == me else T["in%d" % s]

    def tile(r, s):
        return blk(s)[:, _col(r, s):_col(r, s) + TS]

    def bvec(s):
        return blk(s)[:, 0:TK]

    def yv(s):
        return T.ybuf[:, TK * s:TK * (s + 1)]

    def ys(a, b):
        return T.ybuf[:, TK * a:TK * b]

    def bank(r):
        return T["ps%d" % r]

    def ld_of(r):
        return "ld1" if r < LS else ("ld3" if r < L1 else "ld2")

    def ready(q, r, s):
        if s == me:
            wait(q, "ld0" if r is None else ld_of(r), 16)
        elif s == 0 and r is not None and r >= L1:
            wait(q, "a0b", width(s, me))
        elif me == 0 and 2 <= s < LS and r is not None and r >= LS:
            wait(q, "c%d" % s, width(s, me))
        else:
            wait(q, "a%d" % s, width(s, me))

    def block_to(dst, c0, c1, name):
        send(dst, T["in%d" % me][:, c0:c1], T.own[:, c0:c1], name)

    count = {}

    def mm(r, s, rhs, total):
        count[r] = count.get(r, 0) + 1
        g.tensor.matmul(bank(r)[:, 0:TK], tile(r, s), rhs, start=count[r] == 1,
                        stop=count[r] == total).then_inc(sem["mm%d" % r], 1)

    def store(q, src):
        queues[q].dma_start(T.y[:, :], src).then_inc(sem.st, 16)
        wait(q, "st", 16)

    loaded = ["ld0"]
    g.sync.dma_start(T.own[:, 0:TK], T.b[:, :]).then_inc(sem.ld0, 16)
    nld = 0
    for lo, hi in ((1, LS), (LS, L1), (L1, N)):
        r0 = max(lo, me + 1)
        if r0 < hi:
            q = g.scalar if nld % 2 == 0 else g.sync
            nld += 1
            q.dma_start(T.own[:, _col(r0, me):_col(hi, me)], T.l[:, TS * r0:TS * hi]).then_inc(sem[ld_of(r0)], 16)
            loaded.append(ld_of(r0))

    if me == 0:
        wait("g", "ld0", 16)
        wait("g", "ld1", 16)
        block_to(1, 0, _col(2, 0), "a0")
        wait("g", "ld2", 16)
        block_to(1, _col(L1, 0), _col(N, 0), "a0b")
        wait("sc", "ld0", 16)
        store("sc", T.own[:, 0:TK])
        for lo, hi in ((1, LS), (LS, L1)):
            cols = [s for s in (0, 1) if s < lo] + list(range(lo - 1, 1, -1)) + list(range(lo, hi - 1))
            for s in cols:
                for r in range(max(lo, s + 1), hi):
                    ready("t", r, s)
                    if s == 0:
                        ready("t", None, 0)
                        rhs = bvec(0)
                    else:
                        wait("t", "yr%d" % s, 1)
                        rhs = yv(s)
                    mm(r, s, rhs, r)
        for r in range(1, L1):
            ready("v", None, r)
            wait("v", "mm%d" % r, r)
            g.vector.tensor_tensor(yv(r), bvec(r), bank(r)[:, 0:TK], AluOpType.subtract).then_inc(sem["yr%d" % r], 1)
        for lo, hi, name in ((2, LS, "ay"), (LS, L1, "ay2")):
            for r in range(lo, hi):
                wait("g", "yr%d" % r, 1)
            for d in SOLVERS:
                send(d, ys(lo, hi), ys(lo, hi), name)
            for r in range(hi - 1, lo - 1, -1):
                send(r, yv(r), yv(r), "ay")

    elif me == 1:
        wait("g", "ld0", 16)
        wait("g", "ld1", 16)
        wait("g", "ld3", 16)
        block_to(0, 0, _col(L1, 1), "a1")
        nq = N - L1
        ready("t", 1, 0)
        mm(1, 0, bvec(0), 1)
        ready("v", None, 1)
        wait("v", "mm1", 1)
        g.vector.tensor_tensor(yv(1), bvec(1), bank(1)[:, 0:TK], AluOpType.subtract).then_inc(sem.yr1, 1)
        wait("sy", "yr1", 1)
        store("sy", yv(1))
        for r in range(L1, N):
            ready("t", r, 0)
            k = r - L1
            g.tensor.matmul(T.ps2[:, TK * k:TK * (k + 1)], tile(r, 0), bvec(0), start=True, stop=True).then_inc(sem.mq0, 1)
        wait("v", "mq0", nq)
        g.vector.tensor_copy(T.p0[:, :], T.ps2[:, 0:TK * nq]).then_inc(sem.pc, 1)
        wait("t", "yr1", 1)
        for r in range(L1, N):
            ready("t", r, 1)
            k = r - L1
            g.tensor.matmul(T.ps3[:, TK * k:TK * (k + 1)], tile(r, 1), yv(1), start=True, stop=True).then_inc(sem.mq1, 1)
        wait("v", "mq1", nq)
        wait("v", "pc", 1)
        g.vector.tensor_tensor(T.qsrc[:, :], T.p0[:, :], T.ps3[:, 0:TK * nq], AluOpType.add).then_inc(sem.qs, 1)
        wait("g", "qs", 1)
        for d in SOLVERS:
            c = TK * (d - L1 + 1)
            send(d, T.qin[:, 0:c], T.qsrc[:, 0:c], "aq")

    elif me < L1:
        wait("g", "ld0", 16)
        if me < LS:
            if me + 1 < LS:
                wait("g", "ld1", 16)
            block_to(0, 0, _col(LS, me), "a%d" % me)
            wait("g", "ld3", 16)
            block_to(0, _col(LS, me), _col(L1, me), "c%d" % me)
        else:
            if me + 1 < L1:
                wait("g", "ld3", 16)
            block_to(0, 0, _col(L1, me), "a%d" % me)
        wait("g", "ld2", 16)
        for d in SOLVERS:
            block_to(d, _col(L1, me), _col(d + 1, me), "a%d" % me)
        wait("sy", "ay", width(0, me))
        store("sy", yv(me))

    else:
        for d in SOLVERS:
            if d > me:
                wait("g", "ld0", 16)
                wait("g", "ld2", 16)
                block_to(d, 0, _col(d + 1, me), "a%d" % me)
        rows = range(L1, me + 1)
        todo = [(r, s) for s in range(2, LS) for r in rows] + [(r, s) for r in rows for s in range(LS, r)]
        for r, s in todo:
            wait("t", "ay" if s < LS else ("ay2" if s < L1 else "yr%d" % s), width(0, me) if s < L1 else 1)
            ready("t", r, s)
            mm(r, s, yv(s), r - 2)

        def e_op(r):
            k = r - L1
            ready("v", None, r)
            wait("v", "aq", width(1, me))
            g.vector.tensor_tensor(T.ebuf[:, TK * k:TK * (k + 1)], bvec(r), T.qin[:, TK * k:TK * (k + 1)],
                                   AluOpType.subtract).then_inc(sem["er%d" % r], 1)

        def y_op(r):
            k = r - L1
            wait("v", "er%d" % r, 1)
            wait("v", "mm%d" % r, r - 2)
            g.vector.tensor_tensor(yv(r), T.ebuf[:, TK * k:TK * (k + 1)], bank(r)[:, 0:TK],
                                   AluOpType.subtract).then_inc(sem["yr%d" % r], 1)

        e_op(L1)
        for r in rows:
            if r + 1 <= me:
                e_op(r + 1)
            y_op(r)
        wait("sy", "yr%d" % me, 1)
        store("sy", yv(me))

    for name in loaded:
        wait("g", name, 16)
    if sent[0]:
        wait("g", "snt", sent[0])
